import numpy as np
import ml_dtypes


def mxq(x, axis, fmt="e4m3"):
    dtype, down = {"e4m3": (ml_dtypes.float8_e4m3fn, 7), "e5m2": (ml_dtypes.float8_e5m2, 14)}[fmt]
    v = np.moveaxis(np.asarray(x, np.float32).astype(ml_dtypes.bfloat16).astype(np.float64), axis, -1)
    blocks = v.reshape(v.shape[:-1] + (-1, 32))
    amax = np.abs(blocks).max(-1, keepdims=True)
    byte = np.maximum(np.where(amax > 0, np.frexp(amax)[1] - 1 + 127, 0) - down, 1)
    scale = np.exp2(byte - 127.0)
    codes = (blocks / scale).astype(np.float32).astype(dtype).astype(np.float64)
    return np.moveaxis((codes * scale).reshape(v.shape), -1, axis)


WIDE = False


def mx_kscale(k):
    if not WIDE:
        return np.ones(k)
    levels = np.array([10, -10, 5, -5, 0])
    if k % 512:
        return np.exp2(np.random.permutation(np.resize(levels, k // 32))).repeat(32)
    a = np.empty((k // 512, 16))
    for p in range(k // 512):
        a[p, :8] = np.random.permutation(np.resize(levels, 8))
        for g in range(8):
            far = levels[np.abs(levels - a[p, g]) >= 10]
            a[p, g + 8] = far[np.random.randint(len(far))]
    return np.exp2(a.ravel()).repeat(32)


def f64(x):
    return np.asarray(x).astype(np.float64)


def split(x):
    m, e = np.frexp(f64(x))
    hi = np.ldexp(np.trunc(16.0 * m) / 16.0, e)
    return hi, f64(x) - hi


K, M, T = 512, 1536, 512


def setup_inputs():
    n = np.random.standard_normal
    s = mx_kscale(K)[:, None]
    return {
        "w": (n((K, M)) / np.sqrt(K) / s).astype(np.float32),
        "x": (n((K, T)) * s).astype(np.float32),
        "g": (n((1536, 512))).astype(np.float32),
    }


def reference(w, x, g):
    w_hi, w_lo = split(w)
    w_hi_, w_lo_ = mxq(w_hi, 0, "e4m3"), mxq(w_lo, 0, "e4m3")
    x_hi, x_lo = split(x)
    x_hi_, x_lo_ = mxq(x_hi, 0, "e4m3"), mxq(x_lo, 0, "e4m3")
    y = w_hi_.T @ x_hi_ + w_hi_.T @ x_lo_ + w_lo_.T @ x_hi_
    return f64(g) * y

@@ -1,0 +1,168 @@
+from contextlib import ExitStack
+
+import concourse.mybir as mybir
+
+K, M, T = 512, 1536, 512
+FLOPS = 3 * 2 * K * M * T
+
+F32 = mybir.dt.float32
+BF16 = mybir.dt.bfloat16
+I32 = mybir.dt.int32
+U32 = mybir.dt.uint32
+U8 = mybir.dt.uint8
+FP8X4 = mybir.dt.float8_e4m3fn_x4
+ALU = mybir.AluOpType
+
+P = 128
+PACK = 4
+HI_MASK = -983056
+
+X_WIDTHS = (128, 128, 256)
+W_WIDTHS = (256, 256, 256, 256, 256, 128, 128)
+
+
+def top_halves(raw):
+    return raw[:].bitcast(BF16)[:, :, 1::2].rearrange("p t (c i) -> p c t i", i=4)
+
+
+def grouped(part):
+    return part.rearrange("p (c i) t -> p c t i", i=4)
+
+
+def tile_mix_split3_fm_mul_kernel(tc, w, x, g, out):
+    nc = tc.nc
+    n_tiles = M // P
+
+    with ExitStack() as ctx:
+        keep = ctx.enter_context(tc.tile_pool(name="keep", bufs=1))
+        psum = ctx.enter_context(tc.psum_pool(name="psum", bufs=8))
+        ctx.enter_context(tc.manual_schedule())
+
+        warm = keep.tile([P, 2], F32, name="warm")
+        nc.vector.memset(warm[:], 0.0)
+        nc.scalar.copy(out=warm[:, 1:2], in_=warm[:, 0:1])
+
+        x_codes = keep.tile([P, 2, T], U32, name="x_codes", align_bytes=64)
+        x_scales = keep.tile([P, 2, T], U8, name="x_scales", align_bytes=64)
+
+        pieces = []
+        c0 = 0
+        for i, width in enumerate(X_WIDTHS):
+            raw = keep.tile([P, PACK, width], F32, name="x_raw_%d" % i, align_bytes=64)
+            parts = keep.tile([P, 2, width, PACK], BF16, name="x_parts_%d" % i, align_bytes=64)
+            pieces.append((raw, parts, width, c0, False, x_codes, x_scales))
+            c0 += width
+        c0 = 0
+        for i, width in enumerate(W_WIDTHS):
+            raw = keep.tile([P, PACK, width], F32, name="w_raw_%d" % i, align_bytes=64)
+            parts = keep.tile([P, 2, width, PACK], BF16, name="w_parts_%d" % i, align_bytes=64)
+            codes = keep.tile([P, 2, width], U32, name="w_codes_%d" % i, align_bytes=64)
+            scales = keep.tile([P, 2, width], U8, name="w_scales_%d" % i, align_bytes=64)
+            pieces.append((raw, parts, width, c0, True, codes, scales))
+            c0 += width
+        g_tiles = []
+        for i in range(n_tiles // 2):
+            g_pair = keep.tile([P, 2, T], F32, name="g_%d" % i, align_bytes=64)
+            g_tiles.append(g_pair)
+
+        x_rows = x.rearrange("(p j) c -> p j c", j=PACK)
+        w_rows = w.rearrange("(p j) c -> p j c", j=PACK)
+        g_rows = g.rearrange("(b m p) t -> b p m t", m=2, p=P)
+
+        def load_piece(piece):
+            raw, parts, width, col, is_w, codes, scales = piece
+            src = w_rows if is_w else x_rows
+            nc.sync.dma_start(out=raw[:], in_=src[:, :, col : col + width])
+
+        def load_g(i):
+            nc.sync.dma_start(out=g_tiles[i][:], in_=g_rows[i])
+
+        def take_top(piece, on_vector):
+            raw, parts = piece[0], piece[1]
+            if on_vector:
+                nc.vector.tensor_copy(out=grouped(parts[:, 0]), in_=top_halves(raw))
+            else:
+                nc.scalar.copy(out=grouped(parts[:, 0]), in_=top_halves(raw))
+
+        def mask_hi(piece):
+            words = piece[1][:, 0].rearrange("p c t -> p (c t)").bitcast(I32)
+            nc.vector.tensor_scalar(out=words, in0=words, scalar1=HI_MASK, scalar2=None, op0=ALU.bitwise_and)
+
+        def subtract(piece):
+            raw, parts = piece[0], piece[1]
+            nc.vector.tensor_tensor(
+                out=grouped(parts[:, 1]),
+                in0=raw[:].rearrange("p t (c i) -> p c t i", i=4),
+                in1=grouped(parts[:, 0]),
+                op=ALU.subtract,
+            )
+
+        def quantize(piece):
+            raw, parts, width, col, is_w, codes, scales = piece
+            if is_w:
+                nc.vector.quantize_mx(
+                    out=codes[:].rearrange("p h c -> p (h c)").bitcast(FP8X4),
+                    scales=scales[:].rearrange("p h c -> p (h c)"),
+                    in_=parts[:].rearrange("p h c t -> p (h c t)"),
+                )
+            else:
+                for h in range(2):
+                    nc.vector.quantize_mx(
+                        out=codes[:, h, col : col + width].bitcast(FP8X4),
+                        scales=scales[:, h, col : col + width],
+                        in_=parts[:, h].rearrange("p c t -> p (c t)"),
+                    )
+
+        def multiply(piece):
+            raw, parts, width, col, is_w, codes, scales = piece
+            accs = []
+            for m in range(width // P):
+                acc = psum.tile([P, T], F32, name="acc")
+                for step, (wh, xh) in enumerate(((0, 0), (0, 1), (1, 0))):
+                    cols = slice(m * P, (m + 1) * P)
+                    nc.tensor.matmul_mx(
+                        out=acc[:],
+                        lhsT=codes[:, wh, cols].bitcast(FP8X4),
+                        lhsT_scale=scales[:, wh, cols],
+                        rhs=x_codes[:, xh].bitcast(FP8X4),
+                        rhs_scale=x_scales[:, xh],
+                        start=(step == 0),
+                        stop=(step == 2),
+                    )
+                accs.append((acc, col // P + m))
+            return accs
+
+        def finish(acc, m):
+            res = keep.tile([P, T], F32, name="res_%d" % m, align_bytes=64)
+            nc.vector.tensor_tensor(out=res[:], in0=acc[:], in1=g_tiles[m // 2][:, m % 2], op=ALU.mult)
+            nc.sync.dma_start(out=out[m * P : (m + 1) * P, :], in_=res[:])
+
+        n_x = len(X_WIDTHS)
+        loads = pieces[: n_x + 2]
+        for piece in loads:
+            load_piece(piece)
+        rest = pieces[n_x + 2 :]
+        for i in range(max(len(rest), len(g_tiles))):
+            if i < len(g_tiles):
+                load_g(i)
+            if i < len(rest):
+                load_piece(rest[i])
+
+        for i, piece in enumerate(pieces):
+            take_top(piece, i == 0)
+
+        pending = []
+        mask_hi(pieces[0])
+        for i, piece in enumerate(pieces):
+            subtract(piece)
+            if i + 1 < len(pieces):
+                mask_hi(pieces[i + 1])
+            quantize(piece)
+            done = pending
+            pending = []
+            if piece[4]:
+                pending = multiply(piece)
+            for acc, m in done:
+                finish(acc, m)
+        for acc, m in pending:
+            finish(acc, m)

@@ -16,22 +16,16 @@ ALU = mybir.AluOpType
 P = 128
 PACK = 4
 HI_MASK = -983056
-
-X_WIDTHS = (128, 128, 256)
-W_WIDTHS = (256, 256, 256, 256, 256, 128, 128)
-
-
-def top_halves(raw):
-    return raw[:].bitcast(BF16)[:, :, 1::2].rearrange("p t (c i) -> p c t i", i=4)
-
-
-def grouped(part):
-    return part.rearrange("p (c i) t -> p c t i", i=4)
+XW = 128
+WW = 256
+X_LOADS = (128, 128, 256)
+W_LOADS = (256, 256, 512, 512)
+LAG = 2
 
 
 def tile_mix_split3_fm_mul_kernel(tc, w, x, g, out):
     nc = tc.nc
-    n_tiles = M // P
+    n_w = M // WW
 
     with ExitStack() as ctx:
         keep = ctx.enter_context(tc.tile_pool(name="keep", bufs=1))
@@ -45,108 +39,142 @@ def tile_mix_split3_fm_mul_kernel(tc, w, x, g, out):
         x_codes = keep.tile([P, 2, T], U32, name="x_codes", align_bytes=64)
         x_scales = keep.tile([P, 2, T], U8, name="x_scales", align_bytes=64)
 
-        pieces = []
-        c0 = 0
-        for i, width in enumerate(X_WIDTHS):
-            raw = keep.tile([P, PACK, width], F32, name="x_raw_%d" % i, align_bytes=64)
-            parts = keep.tile([P, 2, width, PACK], BF16, name="x_parts_%d" % i, align_bytes=64)
-            pieces.append((raw, parts, width, c0, False, x_codes, x_scales))
-            c0 += width
-        c0 = 0
-        for i, width in enumerate(W_WIDTHS):
-            raw = keep.tile([P, PACK, width], F32, name="w_raw_%d" % i, align_bytes=64)
-            parts = keep.tile([P, 2, width, PACK], BF16, name="w_parts_%d" % i, align_bytes=64)
-            codes = keep.tile([P, 2, width], U32, name="w_codes_%d" % i, align_bytes=64)
-            scales = keep.tile([P, 2, width], U8, name="w_scales_%d" % i, align_bytes=64)
-            pieces.append((raw, parts, width, c0, True, codes, scales))
-            c0 += width
-        g_tiles = []
-        for i in range(n_tiles // 2):
-            g_pair = keep.tile([P, 2, T], F32, name="g_%d" % i, align_bytes=64)
-            g_tiles.append(g_pair)
-
         x_rows = x.rearrange("(p j) c -> p j c", j=PACK)
         w_rows = w.rearrange("(p j) c -> p j c", j=PACK)
-        g_rows = g.rearrange("(b m p) t -> b p m t", m=2, p=P)
+        g_rows = g.rearrange("(b p m) t -> b p m t", m=2, p=P)
+        out_rows = out.rearrange("(b p m) t -> b p m t", m=2, p=P)
 
-        def load_piece(piece):
-            raw, parts, width, col, is_w, codes, scales = piece
-            src = w_rows if is_w else x_rows
-            nc.sync.dma_start(out=raw[:], in_=src[:, :, col : col + width])
+        def make_raws(widths, name):
+            raws = []
+            for i, width in enumerate(widths):
+                raw = keep.tile([P, PACK, width], F32, name="%s_raw_%d" % (name, i), align_bytes=64)
+                raws.append(raw)
+            return raws
+
+        x_raws = make_raws(X_LOADS, "x")
+        w_raws = make_raws(W_LOADS, "w")
+        g_pairs = []
+        for i in range(n_w):
+            g_pair = keep.tile([P, 2, T], F32, name="g_%d" % i, align_bytes=64)
+            g_pairs.append(g_pair)
+
+        def load_x(i):
+            c0 = sum(X_LOADS[:i])
+            nc.sync.dma_start(out=x_raws[i][:], in_=x_rows[:, :, c0 : c0 + X_LOADS[i]])
+
+        def load_w(i):
+            c0 = sum(W_LOADS[:i])
+            nc.sync.dma_start(out=w_raws[i][:], in_=w_rows[:, :, c0 : c0 + W_LOADS[i]])
 
         def load_g(i):
-            nc.sync.dma_start(out=g_tiles[i][:], in_=g_rows[i])
+            nc.sync.dma_start(out=g_pairs[i][:], in_=g_rows[i])
+
+        pieces = []
+        for raw, width in zip(x_raws, X_LOADS):
+            for c in range(0, width, XW):
+                i = len(pieces)
+                parts = keep.tile([P, 2, XW, PACK], BF16, name="x_parts_%d" % i, align_bytes=64)
+                pieces.append((raw, c, XW, parts, i, False))
+        n_x = len(pieces)
+        w_codes = []
+        w_scales = []
+        for raw, width in zip(w_raws, W_LOADS):
+            for c in range(0, width, WW):
+                i = len(pieces) - n_x
+                parts = keep.tile([P, 2, 2, P, PACK], BF16, name="w_parts_%d" % i, align_bytes=64)
+                codes = keep.tile([P, 2, WW], U32, name="w_codes_%d" % i, align_bytes=64)
+                scales = keep.tile([P, 2, WW], U8, name="w_scales_%d" % i, align_bytes=64)
+                w_codes.append(codes)
+                w_scales.append(scales)
+                pieces.append((raw, c, WW, parts, i, True))
+
+        def part_walk(piece, h):
+            raw, c0, width, parts, i, is_w = piece
+            if is_w:
+                return parts[:, h].rearrange("p m c t -> p c t m")
+            return parts[:, h].rearrange("p (c i) t -> p c t i", i=4)
+
+        def raw_walk(view, is_w):
+            return view.rearrange("p t (c i) -> p c t i", i=2 if is_w else 4)
 
         def take_top(piece, on_vector):
-            raw, parts = piece[0], piece[1]
+            raw, c0, width, parts, i, is_w = piece
+            tops = raw[:].bitcast(BF16)[:, :, 2 * c0 + 1 : 2 * (c0 + width) : 2]
             if on_vector:
-                nc.vector.tensor_copy(out=grouped(parts[:, 0]), in_=top_halves(raw))
+                nc.vector.tensor_copy(out=part_walk(piece, 0), in_=raw_walk(tops, is_w))
             else:
-                nc.scalar.copy(out=grouped(parts[:, 0]), in_=top_halves(raw))
+                nc.scalar.copy(out=part_walk(piece, 0), in_=raw_walk(tops, is_w))
+
+        def flat(piece):
+            if piece[5]:
+                return piece[3][:].rearrange("p h m c t -> p (h m c t)")
+            return piece[3][:].rearrange("p h c t -> p (h c t)")
 
         def mask_hi(piece):
-            words = piece[1][:, 0].rearrange("p c t -> p (c t)").bitcast(I32)
+            words = flat(piece)[:, 0 : PACK * piece[2]].bitcast(I32)
             nc.vector.tensor_scalar(out=words, in0=words, scalar1=HI_MASK, scalar2=None, op0=ALU.bitwise_and)
 
         def subtract(piece):
-            raw, parts = piece[0], piece[1]
+            raw, c0, width, parts, i, is_w = piece
             nc.vector.tensor_tensor(
-                out=grouped(parts[:, 1]),
-                in0=raw[:].rearrange("p t (c i) -> p c t i", i=4),
-                in1=grouped(parts[:, 0]),
+                out=part_walk(piece, 1),
+                in0=raw_walk(raw[:, :, c0 : c0 + width], is_w),
+                in1=part_walk(piece, 0),
                 op=ALU.subtract,
             )
 
         def quantize(piece):
-            raw, parts, width, col, is_w, codes, scales = piece
+            raw, c0, width, parts, i, is_w = piece
             if is_w:
                 nc.vector.quantize_mx(
-                    out=codes[:].rearrange("p h c -> p (h c)").bitcast(FP8X4),
-                    scales=scales[:].rearrange("p h c -> p (h c)"),
-                    in_=parts[:].rearrange("p h c t -> p (h c t)"),
+                    out=w_codes[i][:].rearrange("p h c -> p (h c)").bitcast(FP8X4),
+                    scales=w_scales[i][:].rearrange("p h c -> p (h c)"),
+                    in_=flat(piece),
                 )
             else:
+                n = PACK * width
                 for h in range(2):
                     nc.vector.quantize_mx(
-                        out=codes[:, h, col : col + width].bitcast(FP8X4),
-                        scales=scales[:, h, col : col + width],
-                        in_=parts[:, h].rearrange("p c t -> p (c t)"),
+                        out=x_codes[:, h, i * XW : (i + 1) * XW].bitcast(FP8X4),
+                        scales=x_scales[:, h, i * XW : (i + 1) * XW],
+                        in_=flat(piece)[:, h * n : (h + 1) * n],
                     )
 
-        def multiply(piece):
-            raw, parts, width, col, is_w, codes, scales = piece
+        def multiply(i):
             accs = []
-            for m in range(width // P):
+            for m in range(2):
                 acc = psum.tile([P, T], F32, name="acc")
+                cols = slice(m * P, (m + 1) * P)
                 for step, (wh, xh) in enumerate(((0, 0), (0, 1), (1, 0))):
-                    cols = slice(m * P, (m + 1) * P)
                     nc.tensor.matmul_mx(
                         out=acc[:],
-                        lhsT=codes[:, wh, cols].bitcast(FP8X4),
-                        lhsT_scale=scales[:, wh, cols],
+                        lhsT=w_codes[i][:, wh, cols].bitcast(FP8X4),
+                        lhsT_scale=w_scales[i][:, wh, cols],
                         rhs=x_codes[:, xh].bitcast(FP8X4),
                         rhs_scale=x_scales[:, xh],
                         start=(step == 0),
                         stop=(step == 2),
                     )
-                accs.append((acc, col // P + m))
+                accs.append(acc)
             return accs
 
-        def finish(acc, m):
-            res = keep.tile([P, T], F32, name="res_%d" % m, align_bytes=64)
-            nc.vector.tensor_tensor(out=res[:], in0=acc[:], in1=g_tiles[m // 2][:, m % 2], op=ALU.mult)
-            nc.sync.dma_start(out=out[m * P : (m + 1) * P, :], in_=res[:])
+        def finish(i, accs):
+            res = keep.tile([P, 2, T], F32, name="res_%d" % i, align_bytes=64)
+            for m in range(2):
+                nc.vector.tensor_tensor(out=res[:, m], in0=accs[m][:], in1=g_pairs[i][:, m], op=ALU.mult)
+                if i == n_w - 1:
+                    nc.sync.dma_start(out=out_rows[i, :, m], in_=res[:, m])
+            if i < n_w - 1:
+                nc.sync.dma_start(out=out_rows[i], in_=res[:])
 
-        n_x = len(X_WIDTHS)
-        loads = pieces[: n_x + 2]
-        for piece in loads:
-            load_piece(piece)
-        rest = pieces[n_x + 2 :]
-        for i in range(max(len(rest), len(g_tiles))):
-            if i < len(g_tiles):
-                load_g(i)
-            if i < len(rest):
-                load_piece(rest[i])
+        for i in range(3):
+            load_x(i)
+        for i in range(3):
+            load_w(i)
+        load_g(0)
+        load_w(3)
+        for i in range(1, n_w):
+            load_g(i)
 
         for i, piece in enumerate(pieces):
             take_top(piece, i == 0)
@@ -158,11 +186,9 @@ def tile_mix_split3_fm_mul_kernel(tc, w, x, g, out):
             if i + 1 < len(pieces):
                 mask_hi(pieces[i + 1])
             quantize(piece)
-            done = pending
-            pending = []
-            if piece[4]:
-                pending = multiply(piece)
-            for acc, m in done:
-                finish(acc, m)
-        for acc, m in pending:
-            finish(acc, m)
+            if piece[5]:
+                pending.append((piece[4], multiply(piece[4])))
+            if len(pending) > LAG:
+                finish(*pending.pop(0))
+        for k, accs in pending:
+            finish(k, accs)

@@ -19,8 +19,9 @@ HI_MASK = -983056
 XW = 128
 WW = 256
 X_LOADS = (128, 128, 256)
-W_LOADS = (256, 256, 512, 512)
-LAG = 2
+W_LOADS = (256, 256, 256, 256, 256, 256)
+E_PLAN = ((), (0,), (1, 2), (3, 4), (5, 6), (7, 8, 9, 10, 11))
+GP_C = (0, 0, 24, 48, 48, 48)
 
 
 def tile_mix_split3_fm_mul_kernel(tc, w, x, g, out):
@@ -114,14 +115,26 @@ def tile_mix_split3_fm_mul_kernel(tc, w, x, g, out):
             words = flat(piece)[:, 0 : PACK * piece[2]].bitcast(I32)
             nc.vector.tensor_scalar(out=words, in0=words, scalar1=HI_MASK, scalar2=None, op0=ALU.bitwise_and)
 
-        def subtract(piece):
+        def subtract(piece, engine, first, last):
             raw, c0, width, parts, i, is_w = piece
-            nc.vector.tensor_tensor(
-                out=part_walk(piece, 1),
-                in0=raw_walk(raw[:, :, c0 : c0 + width], is_w),
-                in1=part_walk(piece, 0),
+            run = 2 if is_w else 4
+            if engine is nc.gpsimd:
+                nc.gpsimd.tensor_tensor(
+                    out=parts[:, 1, :, first:last],
+                    in0=raw[:, :, c0 + 2 * first : c0 + 2 * last].rearrange("p t (c m) -> p m c t", m=2),
+                    in1=parts[:, 0, :, first:last],
+                    op=ALU.subtract,
+                )
+                return
+            engine.tensor_tensor(
+                out=part_walk(piece, 1)[:, first:last],
+                in0=raw_walk(raw[:, :, c0 + run * first : c0 + run * last], is_w),
+                in1=part_walk(piece, 0)[:, first:last],
                 op=ALU.subtract,
             )
+
+        def gp_share(i):
+            return GP_C[i - n_x] if i >= n_x else 0
 
         def quantize(piece):
             raw, c0, width, parts, i, is_w = piece
@@ -158,23 +171,32 @@ def tile_mix_split3_fm_mul_kernel(tc, w, x, g, out):
                 accs.append(acc)
             return accs
 
-        def finish(i, accs):
+        res_pairs = []
+        for i in range(n_w):
             res = keep.tile([P, 2, T], F32, name="res_%d" % i, align_bytes=64)
-            for m in range(2):
-                nc.vector.tensor_tensor(out=res[:, m], in0=accs[m][:], in1=g_pairs[i][:, m], op=ALU.mult)
-                if i == n_w - 1:
-                    nc.sync.dma_start(out=out_rows[i, :, m], in_=res[:, m])
-            if i < n_w - 1:
+            res_pairs.append(res)
+
+        def finish(tile, acc):
+            i, m = divmod(tile, 2)
+            res = res_pairs[i]
+            if True:
+                n_cut = 2 if i == n_w - 1 and m == 1 else 1
+                for q in range(n_cut):
+                    cols = slice(q * T // n_cut, (q + 1) * T // n_cut)
+                    nc.vector.tensor_tensor(out=res[:, m, cols], in0=acc[:, cols], in1=g_pairs[i][:, m, cols], op=ALU.mult)
+                    if i == n_w - 1:
+                        nc.sync.dma_start(out=out_rows[i, :, m, cols], in_=res[:, m, cols])
+            if i < n_w - 1 and m == 1:
                 nc.sync.dma_start(out=out_rows[i], in_=res[:])
 
         for i in range(3):
             load_x(i)
         for i in range(3):
             load_w(i)
-        load_g(0)
-        load_w(3)
-        for i in range(1, n_w):
+        for i in range(n_w):
             load_g(i)
+            if i + 3 < n_w:
+                load_w(i + 3)
 
         for i, piece in enumerate(pieces):
             take_top(piece, i == 0)
@@ -182,13 +204,14 @@ def tile_mix_split3_fm_mul_kernel(tc, w, x, g, out):
         pending = []
         mask_hi(pieces[0])
         for i, piece in enumerate(pieces):
-            subtract(piece)
+            n_c = P if piece[5] else XW // 4
+            subtract(piece, nc.vector, gp_share(i), n_c)
             if i + 1 < len(pieces):
                 mask_hi(pieces[i + 1])
+                if gp_share(i + 1):
+                    subtract(pieces[i + 1], nc.gpsimd, 0, gp_share(i + 1))
             quantize(piece)
             if piece[5]:
-                pending.append((piece[4], multiply(piece[4])))
-            if len(pending) > LAG:
-                finish(*pending.pop(0))
-        for k, accs in pending:
-            finish(k, accs)
+                pending.extend(multiply(piece[4]))
+                for tile in E_PLAN[piece[4]]:
+                    finish(tile, pending[tile])

@@ -15,18 +15,18 @@ ALU = mybir.AluOpType
 
 P = 128
 PACK = 4
-HI_MASK = -983056
+MASK_F32 = -1048576
+MASK_BF16_PAIR = -983056
+X_LOADS = (128, 128, 256)
 XW = 128
 WW = 256
-X_LOADS = (128, 128, 256)
-W_LOADS = (256, 256, 256, 256, 256, 256)
-E_PLAN = ((), (0,), (1, 2), (3, 4), (5, 6), (7, 8, 9, 10, 11))
-GP_C = (0, 0, 24, 48, 48, 48)
+N_W = M // WW
+GP_SHARE = (0, 0, 56, 56, 56, 56)
+AFTER_QUANT = ((), (0, 1), (2, 3), (4, 5), (6, 7), (9, 10, 11))
 
 
 def tile_mix_split3_fm_mul_kernel(tc, w, x, g, out):
     nc = tc.nc
-    n_w = M // WW
 
     with ExitStack() as ctx:
         keep = ctx.enter_context(tc.tile_pool(name="keep", bufs=1))
@@ -37,130 +37,123 @@ def tile_mix_split3_fm_mul_kernel(tc, w, x, g, out):
         nc.vector.memset(warm[:], 0.0)
         nc.scalar.copy(out=warm[:, 1:2], in_=warm[:, 0:1])
 
-        x_codes = keep.tile([P, 2, T], U32, name="x_codes", align_bytes=64)
-        x_scales = keep.tile([P, 2, T], U8, name="x_scales", align_bytes=64)
-
         x_rows = x.rearrange("(p j) c -> p j c", j=PACK)
         w_rows = w.rearrange("(p j) c -> p j c", j=PACK)
         g_rows = g.rearrange("(b p m) t -> b p m t", m=2, p=P)
         out_rows = out.rearrange("(b p m) t -> b p m t", m=2, p=P)
 
-        def make_raws(widths, name):
-            raws = []
-            for i, width in enumerate(widths):
-                raw = keep.tile([P, PACK, width], F32, name="%s_raw_%d" % (name, i), align_bytes=64)
-                raws.append(raw)
-            return raws
-
-        x_raws = make_raws(X_LOADS, "x")
-        w_raws = make_raws(W_LOADS, "w")
-        g_pairs = []
-        for i in range(n_w):
+        x_parts = keep.tile([P, 2, T, PACK], BF16, name="x_parts", align_bytes=64)
+        x_codes = keep.tile([P, 2, T], U32, name="x_codes", align_bytes=64)
+        x_scales = keep.tile([P, 2, T], U8, name="x_scales", align_bytes=64)
+        x0_hi = keep.tile([P, PACK, XW], F32, name="x0_hi", align_bytes=64)
+        x_raws = []
+        for i, width in enumerate(X_LOADS):
+            raw = keep.tile([P, PACK, width], F32, name="x_raw_%d" % i, align_bytes=64)
+            x_raws.append(raw)
+        w_raws, w_parts, w_codes, w_scales, g_pairs, res_pairs = [], [], [], [], [], []
+        for i in range(N_W):
+            raw = keep.tile([P, PACK, WW], F32, name="w_raw_%d" % i, align_bytes=64)
+            parts = keep.tile([P, 2, 2, P, PACK], BF16, name="w_parts_%d" % i, align_bytes=64)
+            codes = keep.tile([P, 2, WW], U32, name="w_codes_%d" % i, align_bytes=64)
+            scales = keep.tile([P, 2, WW], U8, name="w_scales_%d" % i, align_bytes=64)
             g_pair = keep.tile([P, 2, T], F32, name="g_%d" % i, align_bytes=64)
+            res = keep.tile([P, 2, T], F32, name="res_%d" % i, align_bytes=64)
+            w_raws.append(raw)
+            w_parts.append(parts)
+            w_codes.append(codes)
+            w_scales.append(scales)
             g_pairs.append(g_pair)
+            res_pairs.append(res)
 
-        def load_x(i):
-            c0 = sum(X_LOADS[:i])
-            nc.sync.dma_start(out=x_raws[i][:], in_=x_rows[:, :, c0 : c0 + X_LOADS[i]])
+        def x_raw(i):
+            if i < 2:
+                return x_raws[i][:]
+            return x_raws[2][:, :, (i - 2) * XW : (i - 1) * XW]
 
-        def load_w(i):
-            c0 = sum(W_LOADS[:i])
-            nc.sync.dma_start(out=w_raws[i][:], in_=w_rows[:, :, c0 : c0 + W_LOADS[i]])
+        def x_tops(i):
+            if i < 2:
+                return x_raws[i][:].bitcast(BF16)[:, :, 1::2]
+            return x_raws[2][:].bitcast(BF16)[:, :, 2 * (i - 2) * XW + 1 : 2 * (i - 1) * XW : 2]
 
-        def load_g(i):
-            nc.sync.dma_start(out=g_pairs[i][:], in_=g_rows[i])
+        def by_four(view):
+            return view.rearrange("p t (c i) -> p c t i", i=4)
 
-        pieces = []
-        for raw, width in zip(x_raws, X_LOADS):
-            for c in range(0, width, XW):
-                i = len(pieces)
-                parts = keep.tile([P, 2, XW, PACK], BF16, name="x_parts_%d" % i, align_bytes=64)
-                pieces.append((raw, c, XW, parts, i, False))
-        n_x = len(pieces)
-        w_codes = []
-        w_scales = []
-        for raw, width in zip(w_raws, W_LOADS):
-            for c in range(0, width, WW):
-                i = len(pieces) - n_x
-                parts = keep.tile([P, 2, 2, P, PACK], BF16, name="w_parts_%d" % i, align_bytes=64)
-                codes = keep.tile([P, 2, WW], U32, name="w_codes_%d" % i, align_bytes=64)
-                scales = keep.tile([P, 2, WW], U8, name="w_scales_%d" % i, align_bytes=64)
-                w_codes.append(codes)
-                w_scales.append(scales)
-                pieces.append((raw, c, WW, parts, i, True))
+        def x_part(i, h):
+            return x_parts[:, h, i * XW : (i + 1) * XW].rearrange("p (c i) t -> p c t i", i=4)
 
-        def part_walk(piece, h):
-            raw, c0, width, parts, i, is_w = piece
-            if is_w:
-                return parts[:, h].rearrange("p m c t -> p c t m")
-            return parts[:, h].rearrange("p (c i) t -> p c t i", i=4)
+        def x_mask(i):
+            words = x_parts[:, 0, i * XW : (i + 1) * XW].rearrange("p c t -> p (c t)").bitcast(I32)
+            nc.vector.tensor_scalar(out=words, in0=words, scalar1=MASK_BF16_PAIR, scalar2=None, op0=ALU.bitwise_and)
 
-        def raw_walk(view, is_w):
-            return view.rearrange("p t (c i) -> p c t i", i=2 if is_w else 4)
+        def x_quantize(h, first, last):
+            cols = slice(first * XW, last * XW)
+            nc.vector.quantize_mx(
+                out=x_codes[:, h, cols].bitcast(FP8X4),
+                scales=x_scales[:, h, cols],
+                in_=x_parts[:, h, cols].rearrange("p c t -> p (c t)"),
+            )
 
-        def take_top(piece, on_vector):
-            raw, c0, width, parts, i, is_w = piece
-            tops = raw[:].bitcast(BF16)[:, :, 2 * c0 + 1 : 2 * (c0 + width) : 2]
-            if on_vector:
-                nc.vector.tensor_copy(out=part_walk(piece, 0), in_=raw_walk(tops, is_w))
-            else:
-                nc.scalar.copy(out=part_walk(piece, 0), in_=raw_walk(tops, is_w))
+        def x_subtract(i):
+            nc.vector.tensor_tensor(out=x_part(i, 1), in0=by_four(x_raw(i)), in1=x_part(i, 0), op=ALU.subtract)
 
-        def flat(piece):
-            if piece[5]:
-                return piece[3][:].rearrange("p h m c t -> p (h m c t)")
-            return piece[3][:].rearrange("p h c t -> p (h c t)")
+        def by_two(view):
+            return view.rearrange("p t (c m) -> p c t m", m=2)
 
-        def mask_hi(piece):
-            words = flat(piece)[:, 0 : PACK * piece[2]].bitcast(I32)
-            nc.vector.tensor_scalar(out=words, in0=words, scalar1=HI_MASK, scalar2=None, op0=ALU.bitwise_and)
+        def w_part(i, h):
+            return w_parts[i][:, h].rearrange("p m c t -> p c t m")
 
-        def subtract(piece, engine, first, last):
-            raw, c0, width, parts, i, is_w = piece
-            run = 2 if is_w else 4
-            if engine is nc.gpsimd:
-                nc.gpsimd.tensor_tensor(
-                    out=parts[:, 1, :, first:last],
-                    in0=raw[:, :, c0 + 2 * first : c0 + 2 * last].rearrange("p t (c m) -> p m c t", m=2),
-                    in1=parts[:, 0, :, first:last],
-                    op=ALU.subtract,
-                )
-                return
-            engine.tensor_tensor(
-                out=part_walk(piece, 1)[:, first:last],
-                in0=raw_walk(raw[:, :, c0 + run * first : c0 + run * last], is_w),
-                in1=part_walk(piece, 0)[:, first:last],
+        def w_top(i):
+            nc.scalar.copy(out=w_part(i, 0), in_=by_two(w_raws[i][:].bitcast(BF16)[:, :, 1::2]))
+
+        def w_mask(i):
+            words = w_parts[i][:, 0].rearrange("p m c t -> p (m c t)").bitcast(I32)
+            nc.vector.tensor_scalar(out=words, in0=words, scalar1=MASK_BF16_PAIR, scalar2=None, op0=ALU.bitwise_and)
+
+        def w_subtract(i):
+            cut = GP_SHARE[i]
+            nc.vector.tensor_tensor(
+                out=w_part(i, 1)[:, cut:],
+                in0=by_two(w_raws[i][:, :, 2 * cut :]),
+                in1=w_part(i, 0)[:, cut:],
                 op=ALU.subtract,
             )
 
-        def gp_share(i):
-            return GP_C[i - n_x] if i >= n_x else 0
-
-        def quantize(piece):
-            raw, c0, width, parts, i, is_w = piece
-            if is_w:
-                nc.vector.quantize_mx(
-                    out=w_codes[i][:].rearrange("p h c -> p (h c)").bitcast(FP8X4),
-                    scales=w_scales[i][:].rearrange("p h c -> p (h c)"),
-                    in_=flat(piece),
+        def w_subtract_share(i):
+            cut = GP_SHARE[i]
+            if cut:
+                nc.gpsimd.tensor_tensor(
+                    out=w_parts[i][:, 1, :, :cut],
+                    in0=w_raws[i][:, :, : 2 * cut].rearrange("p t (c m) -> p m c t", m=2),
+                    in1=w_parts[i][:, 0, :, :cut],
+                    op=ALU.subtract,
                 )
-            else:
-                n = PACK * width
-                for h in range(2):
-                    nc.vector.quantize_mx(
-                        out=x_codes[:, h, i * XW : (i + 1) * XW].bitcast(FP8X4),
-                        scales=x_scales[:, h, i * XW : (i + 1) * XW],
-                        in_=flat(piece)[:, h * n : (h + 1) * n],
-                    )
 
-        def multiply(i):
-            accs = []
+        def w_quantize(i):
+            nc.vector.quantize_mx(
+                out=w_codes[i][:].rearrange("p h c -> p (h c)").bitcast(FP8X4),
+                scales=w_scales[i][:].rearrange("p h c -> p (h c)"),
+                in_=w_parts[i][:].rearrange("p h m c t -> p (h m c t)"),
+            )
+
+        def w_quantize_half(i, h):
+            nc.vector.quantize_mx(
+                out=w_codes[i][:, h].bitcast(FP8X4),
+                scales=w_scales[i][:, h],
+                in_=w_parts[i][:, h].rearrange("p m c t -> p (m c t)"),
+            )
+
+        accs = []
+
+        def multiply(i, steps):
             for m in range(2):
-                acc = psum.tile([P, T], F32, name="acc")
+                if 0 in steps:
+                    acc = psum.tile([P, T], F32, name="acc")
+                    accs.append(acc)
                 cols = slice(m * P, (m + 1) * P)
-                for step, (wh, xh) in enumerate(((0, 0), (0, 1), (1, 0))):
+                for step in steps:
+                    wh, xh = ((0, 0), (0, 1), (1, 0))[step]
                     nc.tensor.matmul_mx(
-                        out=acc[:],
+                        out=accs[2 * i + m][:],
                         lhsT=w_codes[i][:, wh, cols].bitcast(FP8X4),
                         lhsT_scale=w_scales[i][:, wh, cols],
                         rhs=x_codes[:, xh].bitcast(FP8X4),
@@ -168,50 +161,73 @@ def tile_mix_split3_fm_mul_kernel(tc, w, x, g, out):
                         start=(step == 0),
                         stop=(step == 2),
                     )
-                accs.append(acc)
-            return accs
 
-        res_pairs = []
-        for i in range(n_w):
-            res = keep.tile([P, 2, T], F32, name="res_%d" % i, align_bytes=64)
-            res_pairs.append(res)
-
-        def finish(tile, acc):
+        def finish(tile):
             i, m = divmod(tile, 2)
-            res = res_pairs[i]
-            if True:
-                n_cut = 2 if i == n_w - 1 and m == 1 else 1
-                for q in range(n_cut):
-                    cols = slice(q * T // n_cut, (q + 1) * T // n_cut)
-                    nc.vector.tensor_tensor(out=res[:, m, cols], in0=acc[:, cols], in1=g_pairs[i][:, m, cols], op=ALU.mult)
-                    if i == n_w - 1:
-                        nc.sync.dma_start(out=out_rows[i, :, m, cols], in_=res[:, m, cols])
-            if i < n_w - 1 and m == 1:
-                nc.sync.dma_start(out=out_rows[i], in_=res[:])
+            n_cut = 2 if tile == 2 * N_W - 1 else 1
+            for q in range(n_cut):
+                cols = slice(q * T // n_cut, (q + 1) * T // n_cut)
+                nc.vector.tensor_tensor(
+                    out=res_pairs[i][:, m, cols], in0=accs[tile][:, cols], in1=g_pairs[i][:, m, cols], op=ALU.mult
+                )
+                if i >= N_W - 3:
+                    nc.sync.dma_start(out=out_rows[i, :, m, cols], in_=res_pairs[i][:, m, cols])
+            if i < N_W - 3 and m == 1:
+                nc.sync.dma_start(out=out_rows[i], in_=res_pairs[i][:])
 
-        for i in range(3):
-            load_x(i)
+        def load_w(i):
+            nc.sync.dma_start(out=w_raws[i][:], in_=w_rows[:, :, i * WW : (i + 1) * WW])
+
+        c0 = 0
+        for raw, width in zip(x_raws, X_LOADS):
+            nc.sync.dma_start(out=raw[:], in_=x_rows[:, :, c0 : c0 + width])
+            c0 += width
         for i in range(3):
             load_w(i)
-        for i in range(n_w):
-            load_g(i)
-            if i + 3 < n_w:
+        for i in range(N_W):
+            nc.sync.dma_start(out=g_pairs[i][:], in_=g_rows[i])
+            if i + 3 < N_W:
                 load_w(i + 3)
 
-        for i, piece in enumerate(pieces):
-            take_top(piece, i == 0)
+        nc.vector.tensor_scalar(
+            out=x0_hi[:].bitcast(I32), in0=x_raws[0][:].bitcast(I32), scalar1=MASK_F32, scalar2=None, op0=ALU.bitwise_and
+        )
+        nc.scalar.copy(out=x_part(1, 0), in_=by_four(x_tops(1)))
+        nc.scalar.copy(out=x_part(0, 0), in_=by_four(x0_hi[:]))
+        for i in (2, 3):
+            nc.scalar.copy(out=x_part(i, 0), in_=by_four(x_tops(i)))
+        for i in range(N_W):
+            w_top(i)
 
-        pending = []
-        mask_hi(pieces[0])
-        for i, piece in enumerate(pieces):
-            n_c = P if piece[5] else XW // 4
-            subtract(piece, nc.vector, gp_share(i), n_c)
-            if i + 1 < len(pieces):
-                mask_hi(pieces[i + 1])
-                if gp_share(i + 1):
-                    subtract(pieces[i + 1], nc.gpsimd, 0, gp_share(i + 1))
-            quantize(piece)
-            if piece[5]:
-                pending.extend(multiply(piece[4]))
-                for tile in E_PLAN[piece[4]]:
-                    finish(tile, pending[tile])
+        nc.vector.tensor_tensor(out=x_part(0, 1), in0=by_four(x_raw(0)), in1=by_four(x0_hi[:]), op=ALU.subtract)
+        x_mask(1)
+        x_quantize(1, 0, 1)
+        x_subtract(1)
+        x_mask(2)
+        x_quantize(0, 0, 2)
+        x_subtract(2)
+        x_mask(3)
+        x_quantize(1, 1, 2)
+        x_subtract(3)
+        w_mask(0)
+        x_quantize(0, 2, 4)
+        x_quantize(1, 2, 4)
+        for i in range(N_W):
+            last = i == N_W - 1
+            if i in (0, N_W - 1):
+                w_quantize_half(i, 0)
+                multiply(i, (0, 1))
+            w_subtract(i)
+            if last:
+                finish(2 * i - 2)
+            else:
+                w_mask(i + 1)
+                w_subtract_share(i + 1)
+            if i in (0, N_W - 1):
+                w_quantize_half(i, 1)
+                multiply(i, (2,))
+            else:
+                w_quantize(i)
+                multiply(i, (0, 1, 2))
+            for tile in AFTER_QUANT[i]:
+                finish(tile)

from contextlib import ExitStack

import concourse.mybir as mybir

K, M, T = 512, 1536, 512
FLOPS = 3 * 2 * K * M * T

F32 = mybir.dt.float32
BF16 = mybir.dt.bfloat16
I32 = mybir.dt.int32
U32 = mybir.dt.uint32
U8 = mybir.dt.uint8
FP8X4 = mybir.dt.float8_e4m3fn_x4
ALU = mybir.AluOpType

P = 128
PACK = 4
MASK_F32 = -1048576
MASK_BF16_PAIR = -983056
X_LOADS = (128, 128, 256)
XW = 128
WW = 256
N_W = M // WW
GP_SHARE = (0, 0, 56, 56, 56, 56)
AFTER_QUANT = ((), (0, 1), (2, 3), (4, 5), (6, 7), (9, 10, 11))


def tile_mix_split3_fm_mul_kernel(tc, w, x, g, out):
    nc = tc.nc

    with ExitStack() as ctx:
        keep = ctx.enter_context(tc.tile_pool(name="keep", bufs=1))
        psum = ctx.enter_context(tc.psum_pool(name="psum", bufs=8))
        ctx.enter_context(tc.manual_schedule())

        warm = keep.tile([P, 2], F32, name="warm")
        nc.vector.memset(warm[:], 0.0)
        nc.scalar.copy(out=warm[:, 1:2], in_=warm[:, 0:1])

        x_rows = x.rearrange("(p j) c -> p j c", j=PACK)
        w_rows = w.rearrange("(p j) c -> p j c", j=PACK)
        g_rows = g.rearrange("(b p m) t -> b p m t", m=2, p=P)
        out_rows = out.rearrange("(b p m) t -> b p m t", m=2, p=P)

        x_parts = keep.tile([P, 2, T, PACK], BF16, name="x_parts", align_bytes=64)
        x_codes = keep.tile([P, 2, T], U32, name="x_codes", align_bytes=64)
        x_scales = keep.tile([P, 2, T], U8, name="x_scales", align_bytes=64)
        x0_hi = keep.tile([P, PACK, XW], F32, name="x0_hi", align_bytes=64)
        x_raws = []
        for i, width in enumerate(X_LOADS):
            raw = keep.tile([P, PACK, width], F32, name="x_raw_%d" % i, align_bytes=64)
            x_raws.append(raw)
        w_raws, w_parts, w_codes, w_scales, g_pairs, res_pairs = [], [], [], [], [], []
        for i in range(N_W):
            raw = keep.tile([P, PACK, WW], F32, name="w_raw_%d" % i, align_bytes=64)
            parts = keep.tile([P, 2, 2, P, PACK], BF16, name="w_parts_%d" % i, align_bytes=64)
            codes = keep.tile([P, 2, WW], U32, name="w_codes_%d" % i, align_bytes=64)
            scales = keep.tile([P, 2, WW], U8, name="w_scales_%d" % i, align_bytes=64)
            g_pair = keep.tile([P, 2, T], F32, name="g_%d" % i, align_bytes=64)
            res = keep.tile([P, 2, T], F32, name="res_%d" % i, align_bytes=64)
            w_raws.append(raw)
            w_parts.append(parts)
            w_codes.append(codes)
            w_scales.append(scales)
            g_pairs.append(g_pair)
            res_pairs.append(res)

        def x_raw(i):
            if i < 2:
                return x_raws[i][:]
            return x_raws[2][:, :, (i - 2) * XW : (i - 1) * XW]

        def x_tops(i):
            if i < 2:
                return x_raws[i][:].bitcast(BF16)[:, :, 1::2]
            return x_raws[2][:].bitcast(BF16)[:, :, 2 * (i - 2) * XW + 1 : 2 * (i - 1) * XW : 2]

        def by_four(view):
            return view.rearrange("p t (c i) -> p c t i", i=4)

        def x_part(i, h):
            return x_parts[:, h, i * XW : (i + 1) * XW].rearrange("p (c i) t -> p c t i", i=4)

        def x_mask(i):
            words = x_parts[:, 0, i * XW : (i + 1) * XW].rearrange("p c t -> p (c t)").bitcast(I32)
            nc.vector.tensor_scalar(out=words, in0=words, scalar1=MASK_BF16_PAIR, scalar2=None, op0=ALU.bitwise_and)

        def x_quantize(h, first, last):
            cols = slice(first * XW, last * XW)
            nc.vector.quantize_mx(
                out=x_codes[:, h, cols].bitcast(FP8X4),
                scales=x_scales[:, h, cols],
                in_=x_parts[:, h, cols].rearrange("p c t -> p (c t)"),
            )

        def x_subtract(i):
            nc.vector.tensor_tensor(out=x_part(i, 1), in0=by_four(x_raw(i)), in1=x_part(i, 0), op=ALU.subtract)

        def by_two(view):
            return view.rearrange("p t (c m) -> p c t m", m=2)

        def w_part(i, h):
            return w_parts[i][:, h].rearrange("p m c t -> p c t m")

        def w_top(i):
            nc.scalar.copy(out=w_part(i, 0), in_=by_two(w_raws[i][:].bitcast(BF16)[:, :, 1::2]))

        def w_mask(i):
            words = w_parts[i][:, 0].rearrange("p m c t -> p (m c t)").bitcast(I32)
            nc.vector.tensor_scalar(out=words, in0=words, scalar1=MASK_BF16_PAIR, scalar2=None, op0=ALU.bitwise_and)

        def w_subtract(i):
            cut = GP_SHARE[i]
            nc.vector.tensor_tensor(
                out=w_part(i, 1)[:, cut:],
                in0=by_two(w_raws[i][:, :, 2 * cut :]),
                in1=w_part(i, 0)[:, cut:],
                op=ALU.subtract,
            )

        def w_subtract_share(i):
            cut = GP_SHARE[i]
            if cut:
                nc.gpsimd.tensor_tensor(
                    out=w_parts[i][:, 1, :, :cut],
                    in0=w_raws[i][:, :, : 2 * cut].rearrange("p t (c m) -> p m c t", m=2),
                    in1=w_parts[i][:, 0, :, :cut],
                    op=ALU.subtract,
                )

        def w_quantize(i):
            nc.vector.quantize_mx(
                out=w_codes[i][:].rearrange("p h c -> p (h c)").bitcast(FP8X4),
                scales=w_scales[i][:].rearrange("p h c -> p (h c)"),
                in_=w_parts[i][:].rearrange("p h m c t -> p (h m c t)"),
            )

        def w_quantize_half(i, h):
            nc.vector.quantize_mx(
                out=w_codes[i][:, h].bitcast(FP8X4),
                scales=w_scales[i][:, h],
                in_=w_parts[i][:, h].rearrange("p m c t -> p (m c t)"),
            )

        accs = []

        def multiply(i, steps):
            for m in range(2):
                if 0 in steps:
                    acc = psum.tile([P, T], F32, name="acc")
                    accs.append(acc)
                cols = slice(m * P, (m + 1) * P)
                for step in steps:
                    wh, xh = ((0, 0), (0, 1), (1, 0))[step]
                    nc.tensor.matmul_mx(
                        out=accs[2 * i + m][:],
                        lhsT=w_codes[i][:, wh, cols].bitcast(FP8X4),
                        lhsT_scale=w_scales[i][:, wh, cols],
                        rhs=x_codes[:, xh].bitcast(FP8X4),
                        rhs_scale=x_scales[:, xh],
                        start=(step == 0),
                        stop=(step == 2),
                    )

        def finish(tile):
            i, m = divmod(tile, 2)
            n_cut = 2 if tile == 2 * N_W - 1 else 1
            for q in range(n_cut):
                cols = slice(q * T // n_cut, (q + 1) * T // n_cut)
                nc.vector.tensor_tensor(
                    out=res_pairs[i][:, m, cols], in0=accs[tile][:, cols], in1=g_pairs[i][:, m, cols], op=ALU.mult
                )
                if i >= N_W - 3:
                    nc.sync.dma_start(out=out_rows[i, :, m, cols], in_=res_pairs[i][:, m, cols])
            if i < N_W - 3 and m == 1:
                nc.sync.dma_start(out=out_rows[i], in_=res_pairs[i][:])

        def load_w(i):
            nc.sync.dma_start(out=w_raws[i][:], in_=w_rows[:, :, i * WW : (i + 1) * WW])

        c0 = 0
        for raw, width in zip(x_raws, X_LOADS):
            nc.sync.dma_start(out=raw[:], in_=x_rows[:, :, c0 : c0 + width])
            c0 += width
        for i in range(3):
            load_w(i)
        for i in range(N_W):
            nc.sync.dma_start(out=g_pairs[i][:], in_=g_rows[i])
            if i + 3 < N_W:
                load_w(i + 3)

        nc.vector.tensor_scalar(
            out=x0_hi[:].bitcast(I32), in0=x_raws[0][:].bitcast(I32), scalar1=MASK_F32, scalar2=None, op0=ALU.bitwise_and
        )
        nc.scalar.copy(out=x_part(1, 0), in_=by_four(x_tops(1)))
        nc.scalar.copy(out=x_part(0, 0), in_=by_four(x0_hi[:]))
        for i in (2, 3):
            nc.scalar.copy(out=x_part(i, 0), in_=by_four(x_tops(i)))
        for i in range(N_W):
            w_top(i)

        nc.vector.tensor_tensor(out=x_part(0, 1), in0=by_four(x_raw(0)), in1=by_four(x0_hi[:]), op=ALU.subtract)
        x_mask(1)
        x_quantize(1, 0, 1)
        x_subtract(1)
        x_mask(2)
        x_quantize(0, 0, 2)
        x_subtract(2)
        x_mask(3)
        x_quantize(1, 1, 2)
        x_subtract(3)
        w_mask(0)
        x_quantize(0, 2, 4)
        x_quantize(1, 2, 4)
        for i in range(N_W):
            last = i == N_W - 1
            if i in (0, N_W - 1):
                w_quantize_half(i, 0)
                multiply(i, (0, 1))
            w_subtract(i)
            if last:
                finish(2 * i - 2)
            else:
                w_mask(i + 1)
                w_subtract_share(i + 1)
            if i in (0, N_W - 1):
                w_quantize_half(i, 1)
                multiply(i, (2,))
            else:
                w_quantize(i)
                multiply(i, (0, 1, 2))
            for tile in AFTER_QUANT[i]:
                finish(tile)
